import numpy as np
CORES = [11,27,43,59,75,91,107,123]
N = 8
WIDTHS = [6,48,48,96,24,12,0,0]
OFF = [0,6,54,102,198,222,234,234]
C = 234
def setup_inputs(rng):
    return {"x": rng.standard_normal((N, 128, C), dtype=np.float32)}
def reference(x):
    s = x.sum(axis=0, dtype=np.float64).astype(x.dtype)
    YW = max(WIDTHS)
    y = np.full((N, 128, YW), np.nan, x.dtype)
    for r in range(N):
        y[r][:, :WIDTHS[r]] = s[:, OFF[r]:OFF[r] + WIDTHS[r]]
    return {"y": y}

@@ -1,0 +1,137 @@
+from concourse.bass import DstId, RemoteDMATransfer
+
+CALLS = (
+    (24, (("b", 102, 96, 4, (7, 6, 13, 15)), ("m", 6, 96, 4, (3, 5, 2, 4)))),
+    (12, (("c", 198, 36, 3, (9, 11, 10)), ("z", 0, 12, 1, (1,)))),
+)
+HCORE = 2
+
+SCRATCH = {}
+SEMAPHORES = ["sent", "arr", "res", "st_sy", "st_sc"]
+for _ci in range(len(CALLS)):
+    SCRATCH["land%d" % _ci] = ("dram", [8 * 128, CALLS[_ci][0]], "float32")
+    SEMAPHORES.append("stg%d" % _ci)
+    for _p in CALLS[_ci][1]:
+        SCRATCH["st_" + _p[0]] = ("dram", [128 * _p[3], CALLS[_ci][0]], "float32")
+        SCRATCH["res_" + _p[0]] = ("dram", [128 * _p[3], CALLS[_ci][0]], "float32")
+
+
+def wplan(topo, core, ci):
+    chunks = []
+    for name, a, w, K, chips in CALLS[ci][1]:
+        for j in range(K):
+            chunks.append((name, j, chips[j] * 8 + HCORE))
+    off = len([c for c in chunks if topo.chip(c[2]) != topo.chip(core)])
+    ne = 1
+    while ne * 2 * off <= 8:
+        ne *= 2
+    out = []
+    eng = 0
+    for name, j, h in chunks:
+        if topo.chip(h) == topo.chip(core):
+            out.append((name, j, h, 0xFF00, 8))
+        else:
+            out.append((name, j, h, ((1 << ne) - 1) << eng, ne))
+            eng += ne
+    return out
+
+
+def piece_of(T, r):
+    o = T.tables["OFF"][r]
+    W = T.tables["WIDTHS"][r]
+    for n, pieces in CALLS:
+        for p in pieces:
+            if p[1] <= o and o + W <= p[1] + p[2]:
+                return n, p
+    return None
+
+
+def dests_of(T, name):
+    return [T.cores[r] for r in range(len(T.cores)) if T.tables["WIDTHS"][r] > 0 and piece_of(T, r)[1][0] == name]
+
+
+def fold_engines(topo, h, dests):
+    for d in dests:
+        if topo.chip(d) != topo.chip(h):
+            return 0x00FF, 8
+    return 0xFFFF, 16
+
+
+def rank_program(g, core, T, topo):
+    rank = T.rank_of(core)
+    if rank is not None:
+        qs = [g.sync, g.scalar]
+        for ci in range(len(CALLS)):
+            for i, (name, a, w, K, chips) in enumerate(CALLS[ci][1]):
+                qs[i % 2].dma_start(T["st_" + name][:], T.x[:, a:a + w]).then_inc(T.sem["stg%d" % ci], 16)
+        tot = 0
+        for ci in range(len(CALLS)):
+            g.wait_ge(T.sem["stg%d" % ci], 16 * len(CALLS[ci][1]))
+            trs = []
+            for name, j, h, mask, ne in wplan(topo, core, ci):
+                rid, pid, _se = topo.addr(h)
+                trs.append(RemoteDMATransfer(
+                    dst_ids=[DstId(rid=rid, pnc=pid)], dma_engine_mask=mask, remote_sem=T.sem.arr,
+                    src=T["st_" + name][128 * j:128 * (j + 1), :],
+                    dst=T["land%d" % ci][128 * rank:128 * (rank + 1), :]))
+                tot += ne
+            g.remote_dma_fused(trs, local_sem=T.sem.sent)
+        W = T.tables["WIDTHS"][rank]
+        if W > 0:
+            n, (name, a, w, K, chips) = piece_of(T, rank)
+            lo = T.tables["OFF"][rank] - a
+            hi = lo + W
+            dests = dests_of(T, name)
+            need = 0
+            for j in range(K):
+                need += fold_engines(topo, chips[j] * 8 + HCORE, dests)[1]
+            res = T["res_" + name]
+            parts = []
+            if w == T.y.shape[1] and lo == 0:
+                parts.append((T.y[:, :], res[:, :]))
+            elif w == T.y.shape[1] and lo % n == 0 and W % n == 0:
+                r0 = lo // n
+                parts.append((T.y[0:127, :], res[r0:r0 + 127 * K, :]))
+                parts.append((T.y[127:128, 0:W], res[127 * K + r0:127 * K + r0 + W // n, :]))
+            else:
+                for u in range(K):
+                    s = max(lo, u * n)
+                    e = min(hi, (u + 1) * n)
+                    if s < e:
+                        parts.append((T.y[:, s - lo:e - lo], res[u::K, s - u * n:e - u * n]))
+            sems = [T.sem.st_sy, T.sem.st_sc]
+            cnt = [0, 0]
+            for q in range(min(2, len(parts))):
+                qs[q].wait_ge(T.sem.res, need)
+            for i, (o_ap, i_ap) in enumerate(parts):
+                qs[i % 2].dma_start(o_ap, i_ap).then_inc(sems[i % 2], 16)
+                cnt[i % 2] += 16
+            for q in range(2):
+                if cnt[q]:
+                    qs[q].wait_ge(sems[q], cnt[q])
+        g.wait_ge(T.sem.sent, tot)
+        return
+    for ci in range(len(CALLS)):
+        for name, a, w, K, chips in CALLS[ci][1]:
+            for j in range(K):
+                if chips[j] * 8 + HCORE != core:
+                    continue
+                exp = 0
+                for c in T.cores:
+                    for e in wplan(topo, c, ci):
+                        if e[0] == name and e[1] == j:
+                            exp += e[4]
+                g.wait_ge(T.sem.arr, exp)
+                dests = dests_of(T, name)
+                ids = []
+                for d in dests:
+                    rid, pid, _se = topo.addr(d)
+                    ids.append(DstId(rid=rid, pnc=pid))
+                mask, ne = fold_engines(topo, core, dests)
+                land = T["land%d" % ci]
+                tr = RemoteDMATransfer(
+                    dst_ids=ids, dma_engine_mask=mask, remote_sem=T.sem.res,
+                    srcs=[land[128 * s:128 * (s + 1), :] for s in range(8)],
+                    dsts=[T["res_" + name][128 * j:128 * (j + 1), :] for _d in dests], alu_op=1)
+                g.remote_dma_fused([tr], local_sem=T.sem.sent)
+                g.wait_ge(T.sem.sent, ne)

@@ -1,8 +1,8 @@
 from concourse.bass import DstId, RemoteDMATransfer
 
 CALLS = (
-    (24, (("b", 102, 96, 4, (7, 6, 13, 15)), ("m", 6, 96, 4, (3, 5, 2, 4)))),
-    (12, (("c", 198, 36, 3, (9, 11, 10)), ("z", 0, 12, 1, (1,)))),
+    (24, (("b", 102, 96, 4, (7, 13, 15, 1)), ("m", 6, 96, 4, (3, 5, 9, 11)))),
+    (12, (("c", 198, 36, 3, (8, 10, 12)), ("z", 0, 12, 1, (0,)))),
 )
 HCORE = 2
 

from concourse.bass import DstId, RemoteDMATransfer

CALLS = (
    (24, (("b", 102, 96, 4, (7, 13, 15, 1)), ("m", 6, 96, 4, (3, 5, 9, 11)))),
    (12, (("c", 198, 36, 3, (8, 10, 12)), ("z", 0, 12, 1, (0,)))),
)
HCORE = 2

SCRATCH = {}
SEMAPHORES = ["sent", "arr", "res", "st_sy", "st_sc"]
for _ci in range(len(CALLS)):
    SCRATCH["land%d" % _ci] = ("dram", [8 * 128, CALLS[_ci][0]], "float32")
    SEMAPHORES.append("stg%d" % _ci)
    for _p in CALLS[_ci][1]:
        SCRATCH["st_" + _p[0]] = ("dram", [128 * _p[3], CALLS[_ci][0]], "float32")
        SCRATCH["res_" + _p[0]] = ("dram", [128 * _p[3], CALLS[_ci][0]], "float32")


def wplan(topo, core, ci):
    chunks = []
    for name, a, w, K, chips in CALLS[ci][1]:
        for j in range(K):
            chunks.append((name, j, chips[j] * 8 + HCORE))
    off = len([c for c in chunks if topo.chip(c[2]) != topo.chip(core)])
    ne = 1
    while ne * 2 * off <= 8:
        ne *= 2
    out = []
    eng = 0
    for name, j, h in chunks:
        if topo.chip(h) == topo.chip(core):
            out.append((name, j, h, 0xFF00, 8))
        else:
            out.append((name, j, h, ((1 << ne) - 1) << eng, ne))
            eng += ne
    return out


def piece_of(T, r):
    o = T.tables["OFF"][r]
    W = T.tables["WIDTHS"][r]
    for n, pieces in CALLS:
        for p in pieces:
            if p[1] <= o and o + W <= p[1] + p[2]:
                return n, p
    return None


def dests_of(T, name):
    return [T.cores[r] for r in range(len(T.cores)) if T.tables["WIDTHS"][r] > 0 and piece_of(T, r)[1][0] == name]


def fold_engines(topo, h, dests):
    for d in dests:
        if topo.chip(d) != topo.chip(h):
            return 0x00FF, 8
    return 0xFFFF, 16


def rank_program(g, core, T, topo):
    rank = T.rank_of(core)
    if rank is not None:
        qs = [g.sync, g.scalar]
        for ci in range(len(CALLS)):
            for i, (name, a, w, K, chips) in enumerate(CALLS[ci][1]):
                qs[i % 2].dma_start(T["st_" + name][:], T.x[:, a:a + w]).then_inc(T.sem["stg%d" % ci], 16)
        tot = 0
        for ci in range(len(CALLS)):
            g.wait_ge(T.sem["stg%d" % ci], 16 * len(CALLS[ci][1]))
            trs = []
            for name, j, h, mask, ne in wplan(topo, core, ci):
                rid, pid, _se = topo.addr(h)
                trs.append(RemoteDMATransfer(
                    dst_ids=[DstId(rid=rid, pnc=pid)], dma_engine_mask=mask, remote_sem=T.sem.arr,
                    src=T["st_" + name][128 * j:128 * (j + 1), :],
                    dst=T["land%d" % ci][128 * rank:128 * (rank + 1), :]))
                tot += ne
            g.remote_dma_fused(trs, local_sem=T.sem.sent)
        W = T.tables["WIDTHS"][rank]
        if W > 0:
            n, (name, a, w, K, chips) = piece_of(T, rank)
            lo = T.tables["OFF"][rank] - a
            hi = lo + W
            dests = dests_of(T, name)
            need = 0
            for j in range(K):
                need += fold_engines(topo, chips[j] * 8 + HCORE, dests)[1]
            res = T["res_" + name]
            parts = []
            if w == T.y.shape[1] and lo == 0:
                parts.append((T.y[:, :], res[:, :]))
            elif w == T.y.shape[1] and lo % n == 0 and W % n == 0:
                r0 = lo // n
                parts.append((T.y[0:127, :], res[r0:r0 + 127 * K, :]))
                parts.append((T.y[127:128, 0:W], res[127 * K + r0:127 * K + r0 + W // n, :]))
            else:
                for u in range(K):
                    s = max(lo, u * n)
                    e = min(hi, (u + 1) * n)
                    if s < e:
                        parts.append((T.y[:, s - lo:e - lo], res[u::K, s - u * n:e - u * n]))
            sems = [T.sem.st_sy, T.sem.st_sc]
            cnt = [0, 0]
            for q in range(min(2, len(parts))):
                qs[q].wait_ge(T.sem.res, need)
            for i, (o_ap, i_ap) in enumerate(parts):
                qs[i % 2].dma_start(o_ap, i_ap).then_inc(sems[i % 2], 16)
                cnt[i % 2] += 16
            for q in range(2):
                if cnt[q]:
                    qs[q].wait_ge(sems[q], cnt[q])
        g.wait_ge(T.sem.sent, tot)
        return
    for ci in range(len(CALLS)):
        for name, a, w, K, chips in CALLS[ci][1]:
            for j in range(K):
                if chips[j] * 8 + HCORE != core:
                    continue
                exp = 0
                for c in T.cores:
                    for e in wplan(topo, c, ci):
                        if e[0] == name and e[1] == j:
                            exp += e[4]
                g.wait_ge(T.sem.arr, exp)
                dests = dests_of(T, name)
                ids = []
                for d in dests:
                    rid, pid, _se = topo.addr(d)
                    ids.append(DstId(rid=rid, pnc=pid))
                mask, ne = fold_engines(topo, core, dests)
                land = T["land%d" % ci]
                tr = RemoteDMATransfer(
                    dst_ids=ids, dma_engine_mask=mask, remote_sem=T.sem.res,
                    srcs=[land[128 * s:128 * (s + 1), :] for s in range(8)],
                    dsts=[T["res_" + name][128 * j:128 * (j + 1), :] for _d in dests], alu_op=1)
                g.remote_dma_fused([tr], local_sem=T.sem.sent)
                g.wait_ge(T.sem.sent, ne)
